import numpy as np
import ml_dtypes


def mxq(x, axis, fmt="e4m3"):
    dtype, down = {"e4m3": (ml_dtypes.float8_e4m3fn, 7), "e5m2": (ml_dtypes.float8_e5m2, 14)}[fmt]
    v = np.moveaxis(np.asarray(x, np.float32).astype(ml_dtypes.bfloat16).astype(np.float64), axis, -1)
    blocks = v.reshape(v.shape[:-1] + (-1, 32))
    amax = np.abs(blocks).max(-1, keepdims=True)
    byte = np.maximum(np.where(amax > 0, np.frexp(amax)[1] - 1 + 127, 0) - down, 1)
    scale = np.exp2(byte - 127.0)
    codes = (blocks / scale).astype(np.float32).astype(dtype).astype(np.float64)
    return np.moveaxis((codes * scale).reshape(v.shape), -1, axis)


WIDE = False


def mx_kscale(k):
    if not WIDE:
        return np.ones(k)
    levels = np.array([10, -10, 5, -5, 0])
    if k % 512:
        return np.exp2(np.random.permutation(np.resize(levels, k // 32))).repeat(32)
    a = np.empty((k // 512, 16))
    for p in range(k // 512):
        a[p, :8] = np.random.permutation(np.resize(levels, 8))
        for g in range(8):
            far = levels[np.abs(levels - a[p, g]) >= 10]
            a[p, g + 8] = far[np.random.randint(len(far))]
    return np.exp2(a.ravel()).repeat(32)


def f64(x):
    return np.asarray(x).astype(np.float64)


def striped(idx):
    return np.tile(idx.reshape(-1, 16).T, (8, 1)).astype(np.uint16)


def unstriped(offs):
    return offs[:16].T.reshape(-1).astype(np.int64)


def pack_weight(w):
    k, n = w.shape
    w = f64(np.asarray(w, np.float32).astype(ml_dtypes.bfloat16)).reshape(k // 32, 32, n)
    amax = np.abs(w).max(1)
    byte = np.clip(np.where(amax > 0, np.frexp(amax)[1] - 1 + 127 - 7, 1), 1, 254)
    scaled = (w * np.exp2(127.0 - byte)[:, None, :]).reshape(k, n).astype(np.float32)
    words = np.ascontiguousarray(scaled.reshape(k // 512, 128, 4, n).transpose(0, 1, 3, 2)).astype(ml_dtypes.float8_e4m3fn).view(np.uint8)
    return words, np.ascontiguousarray(byte.astype(np.uint8).reshape(k // 512, 16, n))


def unpack_weight(words, scales):
    g, p, n, _ = words.shape
    vals = np.ascontiguousarray(words).view(ml_dtypes.float8_e4m3fn).astype(np.float64) * np.repeat(np.exp2(scales.astype(np.float64) - 127.0), 8, axis=1)[..., None]
    return vals.transpose(0, 1, 3, 2).reshape(g * 512, n)


K, T, S, N, H, U = 512, 1024, 512, 128, 512, 1024


def setup_inputs():
    n = np.random.standard_normal
    s = mx_kscale(K)[:, None]
    u = mx_kscale(H)
    packed_xT = pack_weight(n((K, T)) * s)
    return {
        "x_words": packed_xT[0],
        "x_scales": packed_xT[1],
        "w1": (n((K, H)) / np.sqrt(K) / s).astype(np.float32),
        "w2": (n((K, H)) / np.sqrt(K) / s).astype(np.float32),
        "cos": (np.random.uniform(-0.8, 1.0, (H, U))).astype(np.float32),
        "unit": (np.random.uniform(0.6, 1.4, (H, 1)) * u[:, None]).astype(np.float32),
        "w3": (n((H, N)) / np.sqrt(H) / u[:, None]).astype(np.float32),
        "offs": striped(np.random.permutation(T)[:S]),
        "la": striped(np.random.permutation(np.concatenate([np.arange(S), np.random.randint(0, S, U - S)]))),
        "lb": striped(np.random.permutation(np.concatenate([np.arange(S), np.random.randint(0, S, U - S)]))),
    }


def reference(x_words, x_scales, w1, w2, cos, unit, w3, offs, la, lb):
    xq = unpack_weight(x_words, x_scales)[:, unstriped(offs)]
    ya = mxq(f64(w1), 0, "e4m3").T @ xq
    amp = np.log(np.exp(ya) + 1.0)
    aa = amp[:, unstriped(la)]
    ab = amp[:, unstriped(lb)]
    yl = mxq(f64(w2), 0, "e4m3").T @ xq
    shp = np.log(np.exp(yl) + 1.0) + 0.4
    sa = shp[:, unstriped(la)]
    sb = shp[:, unstriped(lb)]
    dm = np.sqrt((sa) ** 2 + (sb) ** 2 + 2.0 * ((sa * sb) * f64(cos)) + 0.1)
    exf = np.exp(0.7 * (dm - sa - sb))
    prod = (aa * ab) * exf
    hid = f64(unit) * (prod / dm)
    return mxq(f64(w3), 0, "e4m3").T @ mxq(hid, 0, "e4m3")

@@ -1,0 +1,245 @@
+import math
+from contextlib import ExitStack
+
+import concourse.mybir as mybir
+from concourse.masks import make_identity
+
+F32 = mybir.dt.float32
+BF16 = mybir.dt.bfloat16
+I32 = mybir.dt.int32
+U32 = mybir.dt.uint32
+U16 = mybir.dt.uint16
+U8 = mybir.dt.uint8
+FP8X4 = mybir.dt.float8_e4m3fn_x4
+ACT = mybir.ActivationFunctionType
+ALU = mybir.AluOpType
+
+P = 128
+K, T, S, N, H, U = 512, 1024, 512, 128, 512, 1024
+FLOPS = 2 * (2 * K * H * S + H * N * U)
+TINY = 2.0 ** -60
+HALF = 512
+CHUNKS = (256, 256, 256, 128, 128)
+PLANE_ORDER = (2, 0, 1, 3)
+UNITS_FIRST = 0
+POOL_P = ((2, 0), (0, 0), (2, 1), (0, 1), (1, 1), (1, 0), (3, 0), (3, 1))
+POOL_M = ((2, 0), (0, 0), (2, 1), (0, 1), (1, 1), (1, 0), (3, 0), (3, 1))
+POOL_NL = ()
+S_ON_SCALAR = {(t, h, k) for t, h in ((0, 0), (0, 1), (1, 0)) for k in (0, 1)}
+L_ON_SCALAR = {(1, 0, 0), (1, 0, 1), (0, 1, 0)}
+UNITS = ((2, 0), (0, 0), (2, 1), (0, 1), (1, 1), (1, 0), (3, 0), (3, 1))
+POOL_LAB = ()
+CAST_ON_SCALAR = (0,)
+
+
+def tile_picked_ysgprd_int_p_kernel(tc, x_words, x_scales, w1, w2, cos, unit, w3, offs, la, lb, out):
+    nc = tc.nc
+    with ExitStack() as ctx:
+        keep = ctx.enter_context(tc.tile_pool(name="keep", bufs=1))
+        psum = ctx.enter_context(tc.psum_pool(name="psum", bufs=1))
+        banks = [psum.tile([P, 512], F32, name=f"bank{b}") for b in range(8)]
+
+        offs_t = keep.tile([P, S // 16], U16, name="offs_t")
+        la_t = keep.tile([P, U // 16], U16, name="la_t")
+        lb_t = keep.tile([P, U // 16], U16, name="lb_t")
+        xw = keep.tile([P, T], I32, name="xw")
+        xs = keep.tile([P, T], U8, name="xs")
+        nc.sync.dma_start(offs_t[:], offs)
+        for q in range(4):
+            rows = x_scales[0, 4 * q : 4 * q + 4, :].bitcast(I32).unsqueeze(0).to_broadcast([8, 4, T // 4])
+            (nc.sync if q < 2 else nc.scalar).dma_start(xs[32 * q : 32 * q + 32, :].bitcast(I32), rows)
+        raws = []
+        for wi, w in enumerate((w1, w2)):
+            for hh in range(2):
+                raw = keep.tile([P, 4, 256], F32, name=f"raw{wi}{hh}")
+                nc.sync.dma_start(raw[:], w.rearrange("(p j) c -> p j c", j=4)[:, :, 256 * hh : 256 * hh + 256])
+                raws.append(raw)
+                if len(raws) == 1:
+                    nc.sync.dma_start(xw[:], x_words[0].rearrange("p n t -> p (n t)").bitcast(I32))
+        nc.sync.dma_start(la_t[:], la)
+        nc.sync.dma_start(lb_t[:], lb)
+        unit_t = keep.tile([P, 4], F32, name="unit_t")
+        unit_k = keep.tile([P, 4], F32, name="unit_k")
+        w3raw = keep.tile([P, 4, N], F32, name="w3raw")
+        nc.sync.dma_start(unit_k[:], unit.rearrange("(p j) o -> p (j o)", j=4))
+        with nc.allow_non_contiguous_dma(reason="one value a partition and plane"):
+            nc.sync.dma_start(unit_t[:], unit.rearrange("(t p) o -> p (t o)", p=P))
+        nc.sync.dma_start(w3raw[:], w3.rearrange("(p j) n -> p j n", j=4))
+        cos_t = {}
+        for t in PLANE_ORDER:
+            cos_t[t] = keep.tile([P, U], F32, name=f"cos{t}")
+            nc.sync.dma_start(cos_t[t][:], cos[P * t : P * t + P, :])
+        ident = keep.tile([P, P], F32, name="ident")
+        make_identity(nc, ident[:])
+
+        xg = keep.tile([P, S], U32, name="xg", align_bytes=64)
+        xsg = keep.tile([P, S], U8, name="xsg", align_bytes=64)
+        nc.vector.tensor_copy(xsg[:], xs[:].indirect(offs_t[:]))
+        nc.vector.tensor_copy(xg[:], xw[:].bitcast(U32).indirect(offs_t[:]))
+
+        s_tab = [keep.tile([P, 1536], F32, name="s_tab0"), keep.tile([P, 1536], F32, name="s_tab1")]
+        l_tab = [keep.tile([P, 1536], F32, name="l_tab0"), keep.tile([P, 1536], F32, name="l_tab1")]
+        e_buf = [keep.tile([P, 1028], F32, name="e_buf0"), keep.tile([P, 1024], F32, name="e_buf1")]
+        e_ya = [s_tab[0][:, 1024:1536], s_tab[1][:, 1024:1536], l_tab[0][:, 1024:1536], l_tab[1][:, 1024:1536]]
+
+        def slot(tiles, t):
+            return tiles[t % 2][:, 512 * (t // 2) : 512 * (t // 2) + 512]
+
+        for ci, raw in enumerate(raws):
+            wi, hh = divmod(ci, 2)
+            grouped = keep.tile([P, 256, 4], BF16, name=f"grouped{ci}", align_bytes=64)
+            dst = grouped[:].rearrange("p (c i) j -> p c j i", i=4)
+            src = raw[:].rearrange("p j (c i) -> p c j i", i=4)
+            if ci in CAST_ON_SCALAR:
+                nc.scalar.copy(dst, src)
+            else:
+                nc.vector.tensor_copy(dst, src)
+            codes = keep.tile([P, 256], U32, name=f"codes{ci}", align_bytes=64)
+            scales = keep.tile([P, 256], U8, name=f"scales{ci}", align_bytes=64)
+            nc.vector.quantize_mx(codes[:].bitcast(FP8X4), scales[:], grouped[:].rearrange("p c j -> p (c j)"))
+            for tt in range(2):
+                t = 2 * hh + tt
+                y = banks[4 * wi + t]
+                nc.tensor.matmul_mx(y[:], codes[:, P * tt : P * tt + P].bitcast(FP8X4), scales[:, P * tt : P * tt + P],
+                                    xg[:].bitcast(FP8X4), xsg[:], start=True, stop=True)
+                nc.scalar.activation(e_ya[t] if wi == 0 else slot(e_buf, t), y[:], ACT.Exp)
+
+        sgn = keep.tile([P, 4], F32, name="sgn")
+        nc.vector.tensor_scalar(sgn[:], unit_k[:], 0.0, 2.0, ALU.is_ge, ALU.mult)
+        nc.vector.tensor_scalar(sgn[:], sgn[:], -1.0, None, ALU.add)
+        nc.vector.scalar_tensor_tensor(e_buf[0][:, 1024:1028], unit_t[:], -1.0, unit_t[:], ALU.mult, ALU.max)
+        w3g = keep.tile([P, N, 4], BF16, name="w3g", align_bytes=64)
+        nc.vector.tensor_tensor(w3g[:], w3raw[:].rearrange("p j n -> p n j"), sgn[:].unsqueeze(1).to_broadcast([P, N, 4]), ALU.mult)
+        w3c = keep.tile([P, N], U32, name="w3c", align_bytes=64)
+        w3s = keep.tile([P, N], U8, name="w3s", align_bytes=64)
+        nc.vector.quantize_mx(w3c[:].bitcast(FP8X4), w3s[:], w3g[:].rearrange("p n j -> p (n j)"))
+        for t, h in POOL_M:
+            cols = slice(HALF * h, HALF * h + HALF)
+            nc.gpsimd.tensor_scalar(cos_t[t][:, cols], cos_t[t][:, cols], -1.0, 1.0, ALU.add, ALU.mult)
+
+        for pair in range(2):
+            nc.scalar.activation(s_tab[pair][:, 0:1024], e_buf[pair][:, 0:1024], ACT.Ln, bias=math.exp(0.4), scale=math.exp(0.4))
+
+        def gather(dst, tiles, t, lst, r0, width, on_scalar):
+            held = tiles[t % 2]
+            window = held[:] if t < 2 else held[:, 512:1536]
+            picked = window.indirect(lst[:, r0 // 16 : (r0 + width) // 16])
+            if on_scalar:
+                nc.scalar.activation(dst, picked, ACT.Copy)
+            else:
+                nc.vector.tensor_copy(dst, picked)
+
+        sa = {t: keep.tile([P, U], F32, name=f"sa{t}") for t in range(4)}
+        sb = {t: keep.tile([P, U], F32, name=f"sb{t}") for t in range(4)}
+        m = {2: keep.tile([P, U], F32, name="m2")[:], 0: keep.tile([P, U], F32, name="m0")[:], 1: keep.tile([P, U], F32, name="m1")[:], 3: l_tab[1][:, 0:1024]}
+        u2 = {(t, h): keep.tile([P, HALF], F32, name=f"u2{t}{h}") for t, h in UNITS}
+        d2 = {t: keep.tile([P, U], F32, name=f"d2{t}") for t in range(4)}
+        lnd = keep.tile([P, 4, U], F32, name="lnd")
+        nl = keep.tile([P, 4, U], F32, name="nl")
+        late = {(2, 0): (m[0][:, 0:HALF], m[0][:, HALF:U]), (0, 0): (m[1][:, HALF:U], m[1][:, 0:HALF]), (2, 1): (d2[3][:, 0:HALF], d2[3][:, HALF:U]), (0, 1): (d2[1][:, 0:HALF], d2[1][:, HALF:U])}
+
+        def s_gathers(t, h):
+            cols = slice(HALF * h, HALF * h + HALF)
+            gather(sa[t][:, cols], s_tab, t, la_t, HALF * h, HALF, (t, h, 0) in S_ON_SCALAR)
+            gather(sb[t][:, cols], s_tab, t, lb_t, HALF * h, HALF, (t, h, 1) in S_ON_SCALAR)
+
+        def unit_chain(t, h):
+            cols = slice(HALF * h, HALF * h + HALF)
+            engine = nc.gpsimd if (t, h) in POOL_P else nc.vector
+            engine.tensor_tensor(m[t][:, cols], sa[t][:, cols], sb[t][:, cols], ALU.mult)
+            if (t, h) in POOL_M:
+                nc.gpsimd.tensor_tensor(m[t][:, cols], cos_t[t][:, cols], m[t][:, cols], ALU.mult)
+            else:
+                nc.vector.scalar_tensor_tensor(m[t][:, cols], cos_t[t][:, cols], -1.0, m[t][:, cols], ALU.add, ALU.mult)
+            bank = banks[UNITS.index((t, h))]
+            for b in range(4):
+                block = slice(HALF * h + P * b, HALF * h + P * b + P)
+                nc.tensor.matmul(bank[:, P * b : P * b + P], sa[t][:, block], ident[:], start=True, stop=False, is_transpose=True)
+                nc.tensor.matmul(bank[:, P * b : P * b + P], sb[t][:, block], ident[:], start=False, stop=True, is_transpose=True)
+            nc.scalar.activation(u2[t, h][:], bank[:], ACT.Square)
+            for b in range(4):
+                nc.tensor.transpose(bank[:, P * b : P * b + P], u2[t, h][:, P * b : P * b + P], ident[:])
+            nc.vector.scalar_tensor_tensor(d2[t][:, cols], m[t][:, cols], 2.0, bank[:], ALU.mult, ALU.add)
+
+        def logs(t):
+            nc.scalar.activation(lnd[:, t, :], d2[t][:], ACT.Ln, bias=0.1)
+            (nc.gpsimd if t in POOL_NL else nc.vector).tensor_scalar(nl[:, t, :], lnd[:, t, :], -0.5, e_buf[0][:, 1024 + t : 1025 + t], ALU.mult, ALU.add)
+
+        def log_tables():
+            for t in range(4):
+                nc.scalar.activation(slot(e_buf, t), e_ya[t], ACT.Ln, bias=1.0)
+            for pair in range(2):
+                nc.scalar.activation(e_buf[pair][:], e_buf[pair][:], ACT.Ln, bias=TINY)
+
+        def l_table(pair):
+            nc.vector.scalar_tensor_tensor(l_tab[pair][:, 0:1024], s_tab[pair][:, 0:1024], -0.7, e_buf[pair][:, 0:1024], ALU.mult, ALU.add)
+
+        def l_gathers(t, h):
+            cols = slice(HALF * h, HALF * h + HALF)
+            homes = late.get((t, h), (sa[t][:, cols], sb[t][:, cols]))
+            for k, lst in enumerate((la_t, lb_t)):
+                gather(homes[k], l_tab, t, lst, HALF * h, HALF, (t, h, k) in L_ON_SCALAR)
+            if (t, h) in POOL_LAB:
+                nc.gpsimd.tensor_tensor(homes[0], homes[0], homes[1], ALU.add)
+            for b in range(4):
+                for term in homes[: 1 if (t, h) in POOL_LAB else 2]:
+                    add_block(term[:, P * b : P * b + P], 4 * h + b, t)
+
+        opened = set()
+
+        def add_block(block, b, t, last=False):
+            nc.tensor.matmul(banks[b][:, P * t : P * t + P], block, ident[:], start=b not in opened, stop=last, is_transpose=True)
+            opened.add(b)
+
+        def add_term(term, b, planes, last=False):
+            for t in planes:
+                add_block(term[:, t, P * b : P * b + P], b, t, last and t == planes[-1])
+
+        def finish(q, r0, width):
+            cols = slice(r0, r0 + width)
+            blocks = range(r0 // P, (r0 + width) // P)
+            nc.scalar.activation(lnd[:, :, cols], lnd[:, :, cols], ACT.Exp, bias=math.log(0.7), scale=0.5)
+            hb = {}
+            for b in blocks:
+                add_term(lnd, b, (0, 1, 2, 3), last=True)
+                hb[b] = keep.tile([P, H], BF16, name=f"hb{b}")
+                nc.scalar.activation(hb[b][:].rearrange("r (u p e) -> r u p e", u=2, e=2),
+                                     banks[b][:].rearrange("r (p u e) -> r u p e", u=2, e=2), ACT.Exp)
+            words = banks[blocks[0]]
+            for i, b in enumerate(blocks):
+                for u in range(2):
+                    nc.tensor.transpose(words[:, P * (2 * i + u) : P * (2 * i + u) + P], hb[b][:].bitcast(F32)[:, P * u : P * u + P], ident[:])
+            hq = keep.tile([P, 4 * width], BF16, name=f"hq{q}", align_bytes=64)
+            nc.vector.tensor_copy(hq[:].bitcast(F32).rearrange("p (b r u) -> p b r u", u=2, r=P),
+                                  words[:, 0 : 2 * width].rearrange("p (b u r) -> p b r u", u=2, r=P))
+            hc = keep.tile([P, width], U32, name=f"hc{q}", align_bytes=64)
+            hs = keep.tile([P, width], U8, name=f"hs{q}", align_bytes=64)
+            nc.vector.quantize_mx(hc[:].bitcast(FP8X4), hs[:], hq[:])
+            res = banks[blocks[0] + 1 if len(blocks) > 1 else blocks[0] - 1]
+            nc.tensor.matmul_mx(res[:, 0:width], w3c[:].bitcast(FP8X4), w3s[:], hc[:].bitcast(FP8X4), hs[:], start=True, stop=True)
+            staged = keep.tile([P, width], F32, name=f"staged{q}")
+            nc.vector.tensor_copy(staged[:], res[:, 0:width])
+            nc.sync.dma_start(out[:, cols], staged[:])
+
+        for t, h in UNITS:
+            s_gathers(t, h)
+        log_tables()
+        for t, h in UNITS:
+            unit_chain(t, h)
+        for t in PLANE_ORDER:
+            logs(t)
+        l_table(0)
+        l_table(1)
+        for t in (2, 0):
+            l_gathers(t, 0)
+        for b in range(8):
+            add_term(nl, b, PLANE_ORDER)
+        for t in (3, 1):
+            l_gathers(t, 0)
+        r0 = 0
+        for q, width in enumerate(CHUNKS):
+            if q == 2:
+                for t in (0, 2, 3, 1):
+                    l_gathers(t, 1)
+            finish(q, r0, width)
+            r0 = r0 + width

@@ -20,15 +20,18 @@ FLOPS = 2 * (2 * K * H * S + H * N * U)
 TINY = 2.0 ** -60
 HALF = 512
 CHUNKS = (256, 256, 256, 128, 128)
-PLANE_ORDER = (2, 0, 1, 3)
+PLANE_ORDER = (2, 0, 3, 1)
 UNITS_FIRST = 0
-POOL_P = ((2, 0), (0, 0), (2, 1), (0, 1), (1, 1), (1, 0), (3, 0), (3, 1))
-POOL_M = ((2, 0), (0, 0), (2, 1), (0, 1), (1, 1), (1, 0), (3, 0), (3, 1))
+POOL_P = ()
+POOL_M = ()
 POOL_NL = ()
-S_ON_SCALAR = {(t, h, k) for t, h in ((0, 0), (0, 1), (1, 0)) for k in (0, 1)}
-L_ON_SCALAR = {(1, 0, 0), (1, 0, 1), (0, 1, 0)}
+S_ON_SCALAR = {(t, h, k) for t in (0, 1) for h in (0, 1) for k in (0, 1)}
+L_ON_SCALAR = {(t, h, k) for t in (0, 1) for h in (0, 1) for k in (0, 1)}
 UNITS = ((2, 0), (0, 0), (2, 1), (0, 1), (1, 1), (1, 0), (3, 0), (3, 1))
 POOL_LAB = ()
+PE_SUM = (2, 0, 3)
+STAGE_ON_SCALAR = (2, 3, 4)
+FUSED = ()
 CAST_ON_SCALAR = (0,)
 
 
@@ -131,35 +134,53 @@ def tile_picked_ysgprd_int_p_kernel(tc, x_words, x_scales, w1, w2, cos, unit, w3
 
         sa = {t: keep.tile([P, U], F32, name=f"sa{t}") for t in range(4)}
         sb = {t: keep.tile([P, U], F32, name=f"sb{t}") for t in range(4)}
-        m = {2: keep.tile([P, U], F32, name="m2")[:], 0: keep.tile([P, U], F32, name="m0")[:], 1: keep.tile([P, U], F32, name="m1")[:], 3: l_tab[1][:, 0:1024]}
-        u2 = {(t, h): keep.tile([P, HALF], F32, name=f"u2{t}{h}") for t, h in UNITS}
+        dm = keep.tile([P, 4, U], F32, name="dm")
+        m = {t: dm[:, t, :] for t in range(4)}
+        u2 = {t: keep.tile([P, U], F32, name=f"u2{t}") for t in range(4)}
         d2 = {t: keep.tile([P, U], F32, name=f"d2{t}") for t in range(4)}
         lnd = keep.tile([P, 4, U], F32, name="lnd")
         nl = keep.tile([P, 4, U], F32, name="nl")
-        late = {(2, 0): (m[0][:, 0:HALF], m[0][:, HALF:U]), (0, 0): (m[1][:, HALF:U], m[1][:, 0:HALF]), (2, 1): (d2[3][:, 0:HALF], d2[3][:, HALF:U]), (0, 1): (d2[1][:, 0:HALF], d2[1][:, HALF:U])}
+        late = {(2, 1): (u2[1][:, 0:HALF], u2[1][:, HALF:U]), (3, 1): (d2[1][:, 0:HALF], d2[1][:, HALF:U])}
 
         def s_gathers(t, h):
             cols = slice(HALF * h, HALF * h + HALF)
             gather(sa[t][:, cols], s_tab, t, la_t, HALF * h, HALF, (t, h, 0) in S_ON_SCALAR)
             gather(sb[t][:, cols], s_tab, t, lb_t, HALF * h, HALF, (t, h, 1) in S_ON_SCALAR)
 
-        def unit_chain(t, h):
-            cols = slice(HALF * h, HALF * h + HALF)
-            engine = nc.gpsimd if (t, h) in POOL_P else nc.vector
-            engine.tensor_tensor(m[t][:, cols], sa[t][:, cols], sb[t][:, cols], ALU.mult)
-            if (t, h) in POOL_M:
-                nc.gpsimd.tensor_tensor(m[t][:, cols], cos_t[t][:, cols], m[t][:, cols], ALU.mult)
-            else:
-                nc.vector.scalar_tensor_tensor(m[t][:, cols], cos_t[t][:, cols], -1.0, m[t][:, cols], ALU.add, ALU.mult)
-            bank = banks[UNITS.index((t, h))]
-            for b in range(4):
-                block = slice(HALF * h + P * b, HALF * h + P * b + P)
-                nc.tensor.matmul(bank[:, P * b : P * b + P], sa[t][:, block], ident[:], start=True, stop=False, is_transpose=True)
-                nc.tensor.matmul(bank[:, P * b : P * b + P], sb[t][:, block], ident[:], start=False, stop=True, is_transpose=True)
-            nc.scalar.activation(u2[t, h][:], bank[:], ACT.Square)
-            for b in range(4):
-                nc.tensor.transpose(bank[:, P * b : P * b + P], u2[t, h][:, P * b : P * b + P], ident[:])
-            nc.vector.scalar_tensor_tensor(d2[t][:, cols], m[t][:, cols], 2.0, bank[:], ALU.mult, ALU.add)
+        def sum_bank(t, h):
+            return banks[7 - 2 * PE_SUM.index(t) - h]
+
+        def products(t):
+            if t not in PE_SUM:
+                nc.vector.tensor_tensor(u2[t][:], sa[t][:], sb[t][:], ALU.add)
+            nc.vector.tensor_tensor(m[t], sa[t][:], sb[t][:], ALU.mult)
+            nc.vector.scalar_tensor_tensor(m[t], cos_t[t][:], -1.0, m[t], ALU.add, ALU.mult)
+
+        def square(t):
+            if t not in PE_SUM:
+                nc.scalar.activation(u2[t][:], u2[t][:], ACT.Square)
+                return
+            for h in range(2):
+                bank = sum_bank(t, h)
+                for b in range(4):
+                    block = slice(HALF * h + P * b, HALF * h + P * b + P)
+                    nc.tensor.matmul(bank[:, P * b : P * b + P], sa[t][:, block], ident[:], start=True, stop=False, is_transpose=True)
+                    nc.tensor.matmul(bank[:, P * b : P * b + P], sb[t][:, block], ident[:], start=False, stop=True, is_transpose=True)
+                nc.scalar.activation(u2[t][:, HALF * h : HALF * h + HALF], bank[:], ACT.Square)
+                for b in range(4):
+                    nc.tensor.transpose(bank[:, P * b : P * b + P], u2[t][:, HALF * h + P * b : HALF * h + P * b + P], ident[:])
+
+        def length(t):
+            if t not in PE_SUM:
+                nc.vector.scalar_tensor_tensor(d2[t][:], m[t], 2.0, u2[t][:], ALU.mult, ALU.add)
+                return
+            for h in range(2):
+                cols = slice(HALF * h, HALF * h + HALF)
+                nc.vector.scalar_tensor_tensor(d2[t][:, cols], m[t][:, cols], 2.0, sum_bank(t, h)[:], ALU.mult, ALU.add)
+
+        def nl_in(t, h):
+            for b in range(4 * h, 4 * h + 4):
+                add_term(nl, b, (t,))
 
         def logs(t):
             nc.scalar.activation(lnd[:, t, :], d2[t][:], ACT.Ln, bias=0.1)
@@ -174,15 +195,21 @@ def tile_picked_ysgprd_int_p_kernel(tc, x_words, x_scales, w1, w2, cos, unit, w3
         def l_table(pair):
             nc.vector.scalar_tensor_tensor(l_tab[pair][:, 0:1024], s_tab[pair][:, 0:1024], -0.7, e_buf[pair][:, 0:1024], ALU.mult, ALU.add)
 
-        def l_gathers(t, h):
+        def l_homes(t, h):
             cols = slice(HALF * h, HALF * h + HALF)
-            homes = late.get((t, h), (sa[t][:, cols], sb[t][:, cols]))
-            for k, lst in enumerate((la_t, lb_t)):
-                gather(homes[k], l_tab, t, lst, HALF * h, HALF, (t, h, k) in L_ON_SCALAR)
-            if (t, h) in POOL_LAB:
-                nc.gpsimd.tensor_tensor(homes[0], homes[0], homes[1], ALU.add)
+            return late.get((t, h), (sa[t][:, cols], sb[t][:, cols]))
+
+        def l_gathers(t, h):
+            homes = l_homes(t, h)
+            gather(homes[0], l_tab, t, la_t, HALF * h, HALF, (t, h, 0) in L_ON_SCALAR)
+            if (t, h) in FUSED:
+                nc.vector.tensor_tensor(homes[1], l_tab[t][:].indirect(lb_t[:, 32 * h : 32 * h + 32]), homes[0], ALU.add)
+            else:
+                gather(homes[1], l_tab, t, lb_t, HALF * h, HALF, (t, h, 1) in L_ON_SCALAR)
+
+        def l_in(t, h):
             for b in range(4):
-                for term in homes[: 1 if (t, h) in POOL_LAB else 2]:
+                for term in l_homes(t, h)[1 if (t, h) in FUSED else 0 :]:
                     add_block(term[:, P * b : P * b + P], 4 * h + b, t)
 
         opened = set()
@@ -198,10 +225,10 @@ def tile_picked_ysgprd_int_p_kernel(tc, x_words, x_scales, w1, w2, cos, unit, w3
         def finish(q, r0, width):
             cols = slice(r0, r0 + width)
             blocks = range(r0 // P, (r0 + width) // P)
-            nc.scalar.activation(lnd[:, :, cols], lnd[:, :, cols], ACT.Exp, bias=math.log(0.7), scale=0.5)
+            nc.scalar.activation(dm[:, :, cols], lnd[:, :, cols], ACT.Exp, bias=math.log(0.7), scale=0.5)
             hb = {}
             for b in blocks:
-                add_term(lnd, b, (0, 1, 2, 3), last=True)
+                add_term(dm, b, (0, 1, 2, 3), last=True)
                 hb[b] = keep.tile([P, H], BF16, name=f"hb{b}")
                 nc.scalar.activation(hb[b][:].rearrange("r (u p e) -> r u p e", u=2, e=2),
                                      banks[b][:].rearrange("r (p u e) -> r u p e", u=2, e=2), ACT.Exp)
@@ -218,28 +245,60 @@ def tile_picked_ysgprd_int_p_kernel(tc, x_words, x_scales, w1, w2, cos, unit, w3
             res = banks[blocks[0] + 1 if len(blocks) > 1 else blocks[0] - 1]
             nc.tensor.matmul_mx(res[:, 0:width], w3c[:].bitcast(FP8X4), w3s[:], hc[:].bitcast(FP8X4), hs[:], start=True, stop=True)
             staged = keep.tile([P, width], F32, name=f"staged{q}")
-            nc.vector.tensor_copy(staged[:], res[:, 0:width])
+            if q in STAGE_ON_SCALAR:
+                nc.scalar.copy(staged[:], res[:, 0:width])
+            else:
+                nc.vector.tensor_copy(staged[:], res[:, 0:width])
             nc.sync.dma_start(out[:, cols], staged[:])
 
-        for t, h in UNITS:
-            s_gathers(t, h)
+        for t in (2, 0, 3):
+            for h in range(2):
+                s_gathers(t, h)
         log_tables()
-        for t, h in UNITS:
-            unit_chain(t, h)
-        for t in PLANE_ORDER:
-            logs(t)
+        products(2)
         l_table(0)
         l_table(1)
-        for t in (2, 0):
-            l_gathers(t, 0)
-        for b in range(8):
-            add_term(nl, b, PLANE_ORDER)
-        for t in (3, 1):
-            l_gathers(t, 0)
+        for t in (2, 0, 3):
+            square(t)
+        for h in range(2):
+            s_gathers(1, h)
+        products(0)
+        length(2)
+        length(0)
+        l_gathers(0, 0)
+        products(3)
+        logs(2)
+        length(3)
+        l_in(0, 0)
+        l_gathers(2, 0)
+        l_in(2, 0)
+        logs(0)
+        products(1)
+        l_gathers(1, 0)
+        logs(3)
+        for h in range(2):
+            for t in (2, 0):
+                nl_in(t, h)
+        l_in(1, 0)
+        l_gathers(3, 0)
+        l_in(3, 0)
+        square(1)
+        l_gathers(0, 1)
+        l_in(0, 1)
+        for h in range(2):
+            nl_in(3, h)
+        l_gathers(1, 1)
+        l_in(1, 1)
+        length(1)
+        logs(1)
+        nl_in(1, 0)
         r0 = 0
         for q, width in enumerate(CHUNKS):
+            if q == 1:
+                nl_in(1, 1)
             if q == 2:
-                for t in (0, 2, 3, 1):
+                for t in (2, 3):
                     l_gathers(t, 1)
+                    l_in(t, 1)
             finish(q, r0, width)
             r0 = r0 + width

@@ -19,7 +19,7 @@ K, T, S, N, H, U = 512, 1024, 512, 128, 512, 1024
 FLOPS = 2 * (2 * K * H * S + H * N * U)
 TINY = 2.0 ** -60
 HALF = 512
-CHUNKS = (256, 256, 256, 128, 128)
+CHUNKS = (128, 256, 256, 256, 128)
 PLANE_ORDER = (2, 0, 3, 1)
 UNITS_FIRST = 0
 POOL_P = ()
@@ -30,9 +30,9 @@ L_ON_SCALAR = {(t, h, k) for t in (0, 1) for h in (0, 1) for k in (0, 1)}
 UNITS = ((2, 0), (0, 0), (2, 1), (0, 1), (1, 1), (1, 0), (3, 0), (3, 1))
 POOL_LAB = ()
 PE_SUM = (2, 0, 3)
-STAGE_ON_SCALAR = (2, 3, 4)
+STAGE_ON_SCALAR = (3, 4)
 FUSED = ()
-CAST_ON_SCALAR = (0,)
+CAST_ON_SCALAR = ()
 
 
 def tile_picked_ysgprd_int_p_kernel(tc, x_words, x_scales, w1, w2, cos, unit, w3, offs, la, lb, out):
@@ -51,13 +51,14 @@ def tile_picked_ysgprd_int_p_kernel(tc, x_words, x_scales, w1, w2, cos, unit, w3
         for q in range(4):
             rows = x_scales[0, 4 * q : 4 * q + 4, :].bitcast(I32).unsqueeze(0).to_broadcast([8, 4, T // 4])
             (nc.sync if q < 2 else nc.scalar).dma_start(xs[32 * q : 32 * q + 32, :].bitcast(I32), rows)
+        nc.sync.dma_start(xw[:], x_words[0].rearrange("p n t -> p (n t)").bitcast(I32))
         raws = []
         for wi, w in enumerate((w1, w2)):
             for hh in range(2):
                 raw = keep.tile([P, 4, 256], F32, name=f"raw{wi}{hh}")
                 nc.sync.dma_start(raw[:], w.rearrange("(p j) c -> p j c", j=4)[:, :, 256 * hh : 256 * hh + 256])
                 raws.append(raw)
-                if len(raws) == 1:
+                if len(raws) == 99:
                     nc.sync.dma_start(xw[:], x_words[0].rearrange("p n t -> p (n t)").bitcast(I32))
         nc.sync.dma_start(la_t[:], la)
         nc.sync.dma_start(lb_t[:], lb)
@@ -82,7 +83,7 @@ def tile_picked_ysgprd_int_p_kernel(tc, x_words, x_scales, w1, w2, cos, unit, w3
 
         s_tab = [keep.tile([P, 1536], F32, name="s_tab0"), keep.tile([P, 1536], F32, name="s_tab1")]
         l_tab = [keep.tile([P, 1536], F32, name="l_tab0"), keep.tile([P, 1536], F32, name="l_tab1")]
-        e_buf = [keep.tile([P, 1028], F32, name="e_buf0"), keep.tile([P, 1024], F32, name="e_buf1")]
+        e_buf = [keep.tile([P, 1024], F32, name="e_buf0"), keep.tile([P, 1024], F32, name="e_buf1")]
         e_ya = [s_tab[0][:, 1024:1536], s_tab[1][:, 1024:1536], l_tab[0][:, 1024:1536], l_tab[1][:, 1024:1536]]
 
         def slot(tiles, t):
@@ -110,7 +111,11 @@ def tile_picked_ysgprd_int_p_kernel(tc, x_words, x_scales, w1, w2, cos, unit, w3
         sgn = keep.tile([P, 4], F32, name="sgn")
         nc.vector.tensor_scalar(sgn[:], unit_k[:], 0.0, 2.0, ALU.is_ge, ALU.mult)
         nc.vector.tensor_scalar(sgn[:], sgn[:], -1.0, None, ALU.add)
-        nc.vector.scalar_tensor_tensor(e_buf[0][:, 1024:1028], unit_t[:], -1.0, unit_t[:], ALU.mult, ALU.max)
+        root = keep.tile([P, 4], F32, name="root")
+        half = keep.tile([P, 4], F32, name="half")
+        nc.gpsimd.memset(half[:], 0.5)
+        nc.vector.scalar_tensor_tensor(unit_t[:], unit_t[:], -1.0, unit_t[:], ALU.mult, ALU.max)
+        nc.gpsimd.tensor_tensor(root[:], unit_t[:], half[:], ALU.pow)
         w3g = keep.tile([P, N, 4], BF16, name="w3g", align_bytes=64)
         nc.vector.tensor_tensor(w3g[:], w3raw[:].rearrange("p j n -> p n j"), sgn[:].unsqueeze(1).to_broadcast([P, N, 4]), ALU.mult)
         w3c = keep.tile([P, N], U32, name="w3c", align_bytes=64)
@@ -139,8 +144,7 @@ def tile_picked_ysgprd_int_p_kernel(tc, x_words, x_scales, w1, w2, cos, unit, w3
         u2 = {t: keep.tile([P, U], F32, name=f"u2{t}") for t in range(4)}
         d2 = {t: keep.tile([P, U], F32, name=f"d2{t}") for t in range(4)}
         lnd = keep.tile([P, 4, U], F32, name="lnd")
-        nl = keep.tile([P, 4, U], F32, name="nl")
-        late = {(2, 1): (u2[1][:, 0:HALF], u2[1][:, HALF:U]), (3, 1): (d2[1][:, 0:HALF], d2[1][:, HALF:U])}
+        late = {(1, 0): (u2[0][:, 0:HALF], u2[0][:, HALF:U]), (2, 1): (u2[1][:, 0:HALF], u2[1][:, HALF:U]), (3, 1): (d2[1][:, 0:HALF], d2[1][:, HALF:U])}
 
         def s_gathers(t, h):
             cols = slice(HALF * h, HALF * h + HALF)
@@ -178,19 +182,14 @@ def tile_picked_ysgprd_int_p_kernel(tc, x_words, x_scales, w1, w2, cos, unit, w3
                 cols = slice(HALF * h, HALF * h + HALF)
                 nc.vector.scalar_tensor_tensor(d2[t][:, cols], m[t][:, cols], 2.0, sum_bank(t, h)[:], ALU.mult, ALU.add)
 
-        def nl_in(t, h):
-            for b in range(4 * h, 4 * h + 4):
-                add_term(nl, b, (t,))
-
         def logs(t):
             nc.scalar.activation(lnd[:, t, :], d2[t][:], ACT.Ln, bias=0.1)
-            (nc.gpsimd if t in POOL_NL else nc.vector).tensor_scalar(nl[:, t, :], lnd[:, t, :], -0.5, e_buf[0][:, 1024 + t : 1025 + t], ALU.mult, ALU.add)
 
         def log_tables():
             for t in range(4):
                 nc.scalar.activation(slot(e_buf, t), e_ya[t], ACT.Ln, bias=1.0)
-            for pair in range(2):
-                nc.scalar.activation(e_buf[pair][:], e_buf[pair][:], ACT.Ln, bias=TINY)
+            for t in (0, 2, 1, 3):
+                nc.scalar.activation(slot(e_buf, t), slot(e_buf, t), ACT.Ln, bias=TINY, scale=root[:, t : t + 1])
 
         def l_table(pair):
             nc.vector.scalar_tensor_tensor(l_tab[pair][:, 0:1024], s_tab[pair][:, 0:1024], -0.7, e_buf[pair][:, 0:1024], ALU.mult, ALU.add)
@@ -222,34 +221,41 @@ def tile_picked_ysgprd_int_p_kernel(tc, x_words, x_scales, w1, w2, cos, unit, w3
             for t in planes:
                 add_block(term[:, t, P * b : P * b + P], b, t, last and t == planes[-1])
 
-        def finish(q, r0, width):
-            cols = slice(r0, r0 + width)
-            blocks = range(r0 // P, (r0 + width) // P)
+        starts = [sum(CHUNKS[:q]) for q in range(len(CHUNKS))]
+
+        def root_term(q):
+            cols = slice(starts[q], starts[q] + CHUNKS[q])
             nc.scalar.activation(dm[:, :, cols], lnd[:, :, cols], ACT.Exp, bias=math.log(0.7), scale=0.5)
+            nc.vector.scalar_tensor_tensor(dm[:, :, cols], lnd[:, :, cols], -0.5, dm[:, :, cols], ALU.mult, ALU.add)
+
+        def hidden(q):
+            blocks = range(starts[q] // P, (starts[q] + CHUNKS[q]) // P)
             hb = {}
             for b in blocks:
                 add_term(dm, b, (0, 1, 2, 3), last=True)
                 hb[b] = keep.tile([P, H], BF16, name=f"hb{b}")
                 nc.scalar.activation(hb[b][:].rearrange("r (u p e) -> r u p e", u=2, e=2),
                                      banks[b][:].rearrange("r (p u e) -> r u p e", u=2, e=2), ACT.Exp)
-            words = banks[blocks[0]]
             for i, b in enumerate(blocks):
                 for u in range(2):
-                    nc.tensor.transpose(words[:, P * (2 * i + u) : P * (2 * i + u) + P], hb[b][:].bitcast(F32)[:, P * u : P * u + P], ident[:])
+                    nc.tensor.transpose(banks[blocks[0]][:, P * (2 * i + u) : P * (2 * i + u) + P], hb[b][:].bitcast(F32)[:, P * u : P * u + P], ident[:])
+
+        def bands(q):
+            width = CHUNKS[q]
+            bank = banks[starts[q] // P]
             hq = keep.tile([P, 4 * width], BF16, name=f"hq{q}", align_bytes=64)
             nc.vector.tensor_copy(hq[:].bitcast(F32).rearrange("p (b r u) -> p b r u", u=2, r=P),
-                                  words[:, 0 : 2 * width].rearrange("p (b u r) -> p b r u", u=2, r=P))
+                                  bank[:, 0 : 2 * width].rearrange("p (b u r) -> p b r u", u=2, r=P))
             hc = keep.tile([P, width], U32, name=f"hc{q}", align_bytes=64)
             hs = keep.tile([P, width], U8, name=f"hs{q}", align_bytes=64)
             nc.vector.quantize_mx(hc[:].bitcast(FP8X4), hs[:], hq[:])
-            res = banks[blocks[0] + 1 if len(blocks) > 1 else blocks[0] - 1]
-            nc.tensor.matmul_mx(res[:, 0:width], w3c[:].bitcast(FP8X4), w3s[:], hc[:].bitcast(FP8X4), hs[:], start=True, stop=True)
+            nc.tensor.matmul_mx(bank[:, 0:width], w3c[:].bitcast(FP8X4), w3s[:], hc[:].bitcast(FP8X4), hs[:], start=True, stop=True)
             staged = keep.tile([P, width], F32, name=f"staged{q}")
             if q in STAGE_ON_SCALAR:
-                nc.scalar.copy(staged[:], res[:, 0:width])
+                nc.scalar.copy(staged[:], bank[:, 0:width])
             else:
-                nc.vector.tensor_copy(staged[:], res[:, 0:width])
-            nc.sync.dma_start(out[:, cols], staged[:])
+                nc.vector.tensor_copy(staged[:], bank[:, 0:width])
+            nc.sync.dma_start(out[:, starts[q] : starts[q] + width], staged[:])
 
         for t in (2, 0, 3):
             for h in range(2):
@@ -265,40 +271,28 @@ def tile_picked_ysgprd_int_p_kernel(tc, x_words, x_scales, w1, w2, cos, unit, w3
         products(0)
         length(2)
         length(0)
-        l_gathers(0, 0)
         products(3)
         logs(2)
         length(3)
-        l_in(0, 0)
-        l_gathers(2, 0)
-        l_in(2, 0)
         logs(0)
-        products(1)
-        l_gathers(1, 0)
+        for t, h in ((0, 0), (2, 0), (1, 0), (3, 0)):
+            l_gathers(t, h)
+            l_in(t, h)
         logs(3)
-        for h in range(2):
-            for t in (2, 0):
-                nl_in(t, h)
-        l_in(1, 0)
-        l_gathers(3, 0)
-        l_in(3, 0)
+        products(1)
         square(1)
-        l_gathers(0, 1)
-        l_in(0, 1)
-        for h in range(2):
-            nl_in(3, h)
-        l_gathers(1, 1)
-        l_in(1, 1)
+        for t, h in ((0, 1), (1, 1)):
+            l_gathers(t, h)
+            l_in(t, h)
         length(1)
         logs(1)
-        nl_in(1, 0)
-        r0 = 0
-        for q, width in enumerate(CHUNKS):
-            if q == 1:
-                nl_in(1, 1)
-            if q == 2:
-                for t in (2, 3):
-                    l_gathers(t, 1)
-                    l_in(t, 1)
-            finish(q, r0, width)
-            r0 = r0 + width
+        for t in (2, 3):
+            l_gathers(t, 1)
+            l_in(t, 1)
+        for step in range(len(CHUNKS) + 2):
+            if step < len(CHUNKS):
+                root_term(step)
+            if 1 <= step <= len(CHUNKS):
+                hidden(step - 1)
+            if step >= 2:
+                bands(step - 2)

@@ -17,22 +17,13 @@ ALU = mybir.AluOpType
 P = 128
 K, T, S, N, H, U = 512, 1024, 512, 128, 512, 1024
 FLOPS = 2 * (2 * K * H * S + H * N * U)
+HALF = U // 2
+W_COLS = 256
 TINY = 2.0 ** -60
-HALF = 512
+EARLY_PLANES = (2, 0, 3)
+LAST_PLANE = 1
 CHUNKS = (128, 256, 256, 256, 128)
-PLANE_ORDER = (2, 0, 3, 1)
-UNITS_FIRST = 0
-POOL_P = ()
-POOL_M = ()
-POOL_NL = ()
-S_ON_SCALAR = {(t, h, k) for t in (0, 1) for h in (0, 1) for k in (0, 1)}
-L_ON_SCALAR = {(t, h, k) for t in (0, 1) for h in (0, 1) for k in (0, 1)}
-UNITS = ((2, 0), (0, 0), (2, 1), (0, 1), (1, 1), (1, 0), (3, 0), (3, 1))
-POOL_LAB = ()
-PE_SUM = (2, 0, 3)
-STAGE_ON_SCALAR = (3, 4)
-FUSED = ()
-CAST_ON_SCALAR = ()
+FIRST_CHUNK_OUT_BY_SCALAR = 2
 
 
 def tile_picked_ysgprd_int_p_kernel(tc, x_words, x_scales, w1, w2, cos, unit, w3, offs, la, lb, out):
@@ -40,7 +31,7 @@ def tile_picked_ysgprd_int_p_kernel(tc, x_words, x_scales, w1, w2, cos, unit, w3
     with ExitStack() as ctx:
         keep = ctx.enter_context(tc.tile_pool(name="keep", bufs=1))
         psum = ctx.enter_context(tc.psum_pool(name="psum", bufs=1))
-        banks = [psum.tile([P, 512], F32, name=f"bank{b}") for b in range(8)]
+        banks = [psum.tile([P, HALF], F32, name=f"bank{b}") for b in range(8)]
 
         offs_t = keep.tile([P, S // 16], U16, name="offs_t")
         la_t = keep.tile([P, U // 16], U16, name="la_t")
@@ -54,12 +45,10 @@ def tile_picked_ysgprd_int_p_kernel(tc, x_words, x_scales, w1, w2, cos, unit, w3
         nc.sync.dma_start(xw[:], x_words[0].rearrange("p n t -> p (n t)").bitcast(I32))
         raws = []
         for wi, w in enumerate((w1, w2)):
-            for hh in range(2):
-                raw = keep.tile([P, 4, 256], F32, name=f"raw{wi}{hh}")
-                nc.sync.dma_start(raw[:], w.rearrange("(p j) c -> p j c", j=4)[:, :, 256 * hh : 256 * hh + 256])
+            for side in range(2):
+                raw = keep.tile([P, 4, W_COLS], F32, name=f"raw{wi}{side}")
+                nc.sync.dma_start(raw[:], w.rearrange("(p j) c -> p j c", j=4)[:, :, W_COLS * side : W_COLS * side + W_COLS])
                 raws.append(raw)
-                if len(raws) == 99:
-                    nc.sync.dma_start(xw[:], x_words[0].rearrange("p n t -> p (n t)").bitcast(I32))
         nc.sync.dma_start(la_t[:], la)
         nc.sync.dma_start(lb_t[:], lb)
         unit_t = keep.tile([P, 4], F32, name="unit_t")
@@ -70,7 +59,7 @@ def tile_picked_ysgprd_int_p_kernel(tc, x_words, x_scales, w1, w2, cos, unit, w3
             nc.sync.dma_start(unit_t[:], unit.rearrange("(t p) o -> p (t o)", p=P))
         nc.sync.dma_start(w3raw[:], w3.rearrange("(p j) n -> p j n", j=4))
         cos_t = {}
-        for t in PLANE_ORDER:
+        for t in EARLY_PLANES + (LAST_PLANE,):
             cos_t[t] = keep.tile([P, U], F32, name=f"cos{t}")
             nc.sync.dma_start(cos_t[t][:], cos[P * t : P * t + P, :])
         ident = keep.tile([P, P], F32, name="ident")
@@ -81,218 +70,195 @@ def tile_picked_ysgprd_int_p_kernel(tc, x_words, x_scales, w1, w2, cos, unit, w3
         nc.vector.tensor_copy(xsg[:], xs[:].indirect(offs_t[:]))
         nc.vector.tensor_copy(xg[:], xw[:].bitcast(U32).indirect(offs_t[:]))
 
-        s_tab = [keep.tile([P, 1536], F32, name="s_tab0"), keep.tile([P, 1536], F32, name="s_tab1")]
-        l_tab = [keep.tile([P, 1536], F32, name="l_tab0"), keep.tile([P, 1536], F32, name="l_tab1")]
-        e_buf = [keep.tile([P, 1024], F32, name="e_buf0"), keep.tile([P, 1024], F32, name="e_buf1")]
-        e_ya = [s_tab[0][:, 1024:1536], s_tab[1][:, 1024:1536], l_tab[0][:, 1024:1536], l_tab[1][:, 1024:1536]]
+        s_tab = [keep.tile([P, 3 * S], F32, name="s_tab0"), keep.tile([P, 3 * S], F32, name="s_tab1")]
+        logf_tab = [keep.tile([P, 3 * S], F32, name="logf_tab0"), keep.tile([P, 3 * S], F32, name="logf_tab1")]
+        work = [keep.tile([P, 2 * S], F32, name="work0"), keep.tile([P, 2 * S], F32, name="work1")]
+        exp_ya = [tab[:, 2 * S : 3 * S] for tab in s_tab + logf_tab]
 
-        def slot(tiles, t):
-            return tiles[t % 2][:, 512 * (t // 2) : 512 * (t // 2) + 512]
+        def work_plane(t):
+            return work[t % 2][:, S * (t // 2) : S * (t // 2) + S]
 
         for ci, raw in enumerate(raws):
-            wi, hh = divmod(ci, 2)
-            grouped = keep.tile([P, 256, 4], BF16, name=f"grouped{ci}", align_bytes=64)
-            dst = grouped[:].rearrange("p (c i) j -> p c j i", i=4)
-            src = raw[:].rearrange("p j (c i) -> p c j i", i=4)
-            if ci in CAST_ON_SCALAR:
-                nc.scalar.copy(dst, src)
-            else:
-                nc.vector.tensor_copy(dst, src)
-            codes = keep.tile([P, 256], U32, name=f"codes{ci}", align_bytes=64)
-            scales = keep.tile([P, 256], U8, name=f"scales{ci}", align_bytes=64)
+            wi, side = divmod(ci, 2)
+            grouped = keep.tile([P, W_COLS, 4], BF16, name=f"grouped{ci}", align_bytes=64)
+            nc.vector.tensor_copy(grouped[:].rearrange("p (c i) j -> p c j i", i=4), raw[:].rearrange("p j (c i) -> p c j i", i=4))
+            codes = keep.tile([P, W_COLS], U32, name=f"codes{ci}", align_bytes=64)
+            scales = keep.tile([P, W_COLS], U8, name=f"scales{ci}", align_bytes=64)
             nc.vector.quantize_mx(codes[:].bitcast(FP8X4), scales[:], grouped[:].rearrange("p c j -> p (c j)"))
-            for tt in range(2):
-                t = 2 * hh + tt
+            for i in range(2):
+                t = 2 * side + i
                 y = banks[4 * wi + t]
-                nc.tensor.matmul_mx(y[:], codes[:, P * tt : P * tt + P].bitcast(FP8X4), scales[:, P * tt : P * tt + P],
+                nc.tensor.matmul_mx(y[:], codes[:, P * i : P * i + P].bitcast(FP8X4), scales[:, P * i : P * i + P],
                                     xg[:].bitcast(FP8X4), xsg[:], start=True, stop=True)
-                nc.scalar.activation(e_ya[t] if wi == 0 else slot(e_buf, t), y[:], ACT.Exp)
+                nc.scalar.activation(exp_ya[t] if wi == 0 else work_plane(t), y[:], ACT.Exp)
 
         sgn = keep.tile([P, 4], F32, name="sgn")
         nc.vector.tensor_scalar(sgn[:], unit_k[:], 0.0, 2.0, ALU.is_ge, ALU.mult)
         nc.vector.tensor_scalar(sgn[:], sgn[:], -1.0, None, ALU.add)
         root = keep.tile([P, 4], F32, name="root")
-        half = keep.tile([P, 4], F32, name="half")
-        nc.gpsimd.memset(half[:], 0.5)
+        one_half = keep.tile([P, 4], F32, name="one_half")
+        nc.gpsimd.memset(one_half[:], 0.5)
         nc.vector.scalar_tensor_tensor(unit_t[:], unit_t[:], -1.0, unit_t[:], ALU.mult, ALU.max)
-        nc.gpsimd.tensor_tensor(root[:], unit_t[:], half[:], ALU.pow)
+        nc.gpsimd.tensor_tensor(root[:], unit_t[:], one_half[:], ALU.pow)
         w3g = keep.tile([P, N, 4], BF16, name="w3g", align_bytes=64)
         nc.vector.tensor_tensor(w3g[:], w3raw[:].rearrange("p j n -> p n j"), sgn[:].unsqueeze(1).to_broadcast([P, N, 4]), ALU.mult)
         w3c = keep.tile([P, N], U32, name="w3c", align_bytes=64)
         w3s = keep.tile([P, N], U8, name="w3s", align_bytes=64)
         nc.vector.quantize_mx(w3c[:].bitcast(FP8X4), w3s[:], w3g[:].rearrange("p n j -> p (n j)"))
-        for t, h in POOL_M:
-            cols = slice(HALF * h, HALF * h + HALF)
-            nc.gpsimd.tensor_scalar(cos_t[t][:, cols], cos_t[t][:, cols], -1.0, 1.0, ALU.add, ALU.mult)
 
         for pair in range(2):
-            nc.scalar.activation(s_tab[pair][:, 0:1024], e_buf[pair][:, 0:1024], ACT.Ln, bias=math.exp(0.4), scale=math.exp(0.4))
+            nc.scalar.activation(s_tab[pair][:, 0 : 2 * S], work[pair][:], ACT.Ln, bias=math.exp(0.4), scale=math.exp(0.4))
 
-        def gather(dst, tiles, t, lst, r0, width, on_scalar):
-            held = tiles[t % 2]
-            window = held[:] if t < 2 else held[:, 512:1536]
-            picked = window.indirect(lst[:, r0 // 16 : (r0 + width) // 16])
+        sa = {t: keep.tile([P, U], F32, name=f"sa{t}") for t in range(4)}
+        sb = {t: keep.tile([P, U], F32, name=f"sb{t}") for t in range(4)}
+        tail = keep.tile([P, 4, U], F32, name="tail")
+        cross = {t: keep.tile([P, U], F32, name="cross_last")[:] if t == LAST_PLANE else tail[:, t, :] for t in range(4)}
+        sq = {t: keep.tile([P, U], F32, name=f"sq{t}") for t in range(4)}
+        d2 = {t: keep.tile([P, U], F32, name=f"d2{t}") for t in range(4)}
+        log_d2 = keep.tile([P, 4, U], F32, name="log_d2")
+
+        def half_cols(h):
+            return slice(HALF * h, HALF * h + HALF)
+
+        def gather(dst, tabs, t, lst, h, on_scalar):
+            window = tabs[t][:] if t < 2 else tabs[t - 2][:, S : 3 * S]
+            picked = window.indirect(lst[:, 32 * h : 32 * h + 32])
             if on_scalar:
                 nc.scalar.activation(dst, picked, ACT.Copy)
             else:
                 nc.vector.tensor_copy(dst, picked)
 
-        sa = {t: keep.tile([P, U], F32, name=f"sa{t}") for t in range(4)}
-        sb = {t: keep.tile([P, U], F32, name=f"sb{t}") for t in range(4)}
-        dm = keep.tile([P, 4, U], F32, name="dm")
-        m = {t: dm[:, t, :] for t in range(4)}
-        u2 = {t: keep.tile([P, U], F32, name=f"u2{t}") for t in range(4)}
-        d2 = {t: keep.tile([P, U], F32, name=f"d2{t}") for t in range(4)}
-        lnd = keep.tile([P, 4, U], F32, name="lnd")
-        late = {(1, 0): (u2[0][:, 0:HALF], u2[0][:, HALF:U]), (2, 1): (u2[1][:, 0:HALF], u2[1][:, HALF:U]), (3, 1): (d2[1][:, 0:HALF], d2[1][:, HALF:U])}
+        def gather_s(t):
+            for h in range(2):
+                gather(sa[t][:, half_cols(h)], s_tab, t, la_t, h, t < 2)
+                gather(sb[t][:, half_cols(h)], s_tab, t, lb_t, h, t < 2)
 
-        def s_gathers(t, h):
-            cols = slice(HALF * h, HALF * h + HALF)
-            gather(sa[t][:, cols], s_tab, t, la_t, HALF * h, HALF, (t, h, 0) in S_ON_SCALAR)
-            gather(sb[t][:, cols], s_tab, t, lb_t, HALF * h, HALF, (t, h, 1) in S_ON_SCALAR)
+        def log_amp():
+            for t in range(4):
+                nc.scalar.activation(work_plane(t), exp_ya[t], ACT.Ln, bias=1.0)
+            for t in (0, 2, 1, 3):
+                nc.scalar.activation(work_plane(t), work_plane(t), ACT.Ln, bias=TINY, scale=root[:, t : t + 1])
+
+        def make_logf(pair):
+            nc.vector.scalar_tensor_tensor(logf_tab[pair][:, 0 : 2 * S], s_tab[pair][:, 0 : 2 * S], -0.7, work[pair][:], ALU.mult, ALU.add)
+
+        def make_cross(t):
+            nc.vector.tensor_tensor(cross[t], sa[t][:], sb[t][:], ALU.mult)
+            nc.vector.scalar_tensor_tensor(cross[t], cos_t[t][:], -1.0, cross[t], ALU.add, ALU.mult)
 
         def sum_bank(t, h):
-            return banks[7 - 2 * PE_SUM.index(t) - h]
+            return banks[2 * EARLY_PLANES.index(t) + h]
 
-        def products(t):
-            if t not in PE_SUM:
-                nc.vector.tensor_tensor(u2[t][:], sa[t][:], sb[t][:], ALU.add)
-            nc.vector.tensor_tensor(m[t], sa[t][:], sb[t][:], ALU.mult)
-            nc.vector.scalar_tensor_tensor(m[t], cos_t[t][:], -1.0, m[t], ALU.add, ALU.mult)
-
-        def square(t):
-            if t not in PE_SUM:
-                nc.scalar.activation(u2[t][:], u2[t][:], ACT.Square)
-                return
+        def square_early(t):
             for h in range(2):
                 bank = sum_bank(t, h)
                 for b in range(4):
                     block = slice(HALF * h + P * b, HALF * h + P * b + P)
                     nc.tensor.matmul(bank[:, P * b : P * b + P], sa[t][:, block], ident[:], start=True, stop=False, is_transpose=True)
                     nc.tensor.matmul(bank[:, P * b : P * b + P], sb[t][:, block], ident[:], start=False, stop=True, is_transpose=True)
-                nc.scalar.activation(u2[t][:, HALF * h : HALF * h + HALF], bank[:], ACT.Square)
+                nc.scalar.activation(sq[t][:, half_cols(h)], bank[:], ACT.Square)
                 for b in range(4):
-                    nc.tensor.transpose(bank[:, P * b : P * b + P], u2[t][:, HALF * h + P * b : HALF * h + P * b + P], ident[:])
+                    nc.tensor.transpose(bank[:, P * b : P * b + P], sq[t][:, HALF * h + P * b : HALF * h + P * b + P], ident[:])
 
-        def length(t):
-            if t not in PE_SUM:
-                nc.vector.scalar_tensor_tensor(d2[t][:], m[t], 2.0, u2[t][:], ALU.mult, ALU.add)
-                return
+        def d2_early(t):
             for h in range(2):
-                cols = slice(HALF * h, HALF * h + HALF)
-                nc.vector.scalar_tensor_tensor(d2[t][:, cols], m[t][:, cols], 2.0, sum_bank(t, h)[:], ALU.mult, ALU.add)
+                nc.vector.scalar_tensor_tensor(d2[t][:, half_cols(h)], cross[t][:, half_cols(h)], 2.0, sum_bank(t, h)[:], ALU.mult, ALU.add)
 
-        def logs(t):
-            nc.scalar.activation(lnd[:, t, :], d2[t][:], ACT.Ln, bias=0.1)
-
-        def log_tables():
-            for t in range(4):
-                nc.scalar.activation(slot(e_buf, t), e_ya[t], ACT.Ln, bias=1.0)
-            for t in (0, 2, 1, 3):
-                nc.scalar.activation(slot(e_buf, t), slot(e_buf, t), ACT.Ln, bias=TINY, scale=root[:, t : t + 1])
-
-        def l_table(pair):
-            nc.vector.scalar_tensor_tensor(l_tab[pair][:, 0:1024], s_tab[pair][:, 0:1024], -0.7, e_buf[pair][:, 0:1024], ALU.mult, ALU.add)
-
-        def l_homes(t, h):
-            cols = slice(HALF * h, HALF * h + HALF)
-            return late.get((t, h), (sa[t][:, cols], sb[t][:, cols]))
-
-        def l_gathers(t, h):
-            homes = l_homes(t, h)
-            gather(homes[0], l_tab, t, la_t, HALF * h, HALF, (t, h, 0) in L_ON_SCALAR)
-            if (t, h) in FUSED:
-                nc.vector.tensor_tensor(homes[1], l_tab[t][:].indirect(lb_t[:, 32 * h : 32 * h + 32]), homes[0], ALU.add)
-            else:
-                gather(homes[1], l_tab, t, lb_t, HALF * h, HALF, (t, h, 1) in L_ON_SCALAR)
-
-        def l_in(t, h):
-            for b in range(4):
-                for term in l_homes(t, h)[1 if (t, h) in FUSED else 0 :]:
-                    add_block(term[:, P * b : P * b + P], 4 * h + b, t)
+        def take_log(t):
+            nc.scalar.activation(log_d2[:, t, :], d2[t][:], ACT.Ln, bias=0.1)
 
         opened = set()
 
-        def add_block(block, b, t, last=False):
-            nc.tensor.matmul(banks[b][:, P * t : P * t + P], block, ident[:], start=b not in opened, stop=last, is_transpose=True)
+        def add_turned(term, b, t, last):
+            nc.tensor.matmul(banks[b][:, P * t : P * t + P], term, ident[:], start=b not in opened, stop=last, is_transpose=True)
             opened.add(b)
 
-        def add_term(term, b, planes, last=False):
-            for t in planes:
-                add_block(term[:, t, P * b : P * b + P], b, t, last and t == planes[-1])
+        def add_logf(t, h, room):
+            gather(room[0], logf_tab, t, la_t, h, t < 2)
+            gather(room[1], logf_tab, t, lb_t, h, t < 2 and (t, h) != (LAST_PLANE, 1))
+            for b in range(4):
+                for term in room:
+                    add_turned(term[:, P * b : P * b + P], 4 * h + b, t, False)
+
+        def own_room(t, h):
+            return sa[t][:, half_cols(h)], sb[t][:, half_cols(h)]
+
+        def halves(region):
+            return region[:, half_cols(0)], region[:, half_cols(1)]
 
         starts = [sum(CHUNKS[:q]) for q in range(len(CHUNKS))]
 
-        def root_term(q):
+        def make_tail(q):
             cols = slice(starts[q], starts[q] + CHUNKS[q])
-            nc.scalar.activation(dm[:, :, cols], lnd[:, :, cols], ACT.Exp, bias=math.log(0.7), scale=0.5)
-            nc.vector.scalar_tensor_tensor(dm[:, :, cols], lnd[:, :, cols], -0.5, dm[:, :, cols], ALU.mult, ALU.add)
+            nc.scalar.activation(tail[:, :, cols], log_d2[:, :, cols], ACT.Exp, bias=math.log(0.7), scale=0.5)
+            nc.vector.scalar_tensor_tensor(tail[:, :, cols], log_d2[:, :, cols], -0.5, tail[:, :, cols], ALU.mult, ALU.add)
 
-        def hidden(q):
+        def make_hidden(q):
             blocks = range(starts[q] // P, (starts[q] + CHUNKS[q]) // P)
-            hb = {}
+            hid_t = {}
             for b in blocks:
-                add_term(dm, b, (0, 1, 2, 3), last=True)
-                hb[b] = keep.tile([P, H], BF16, name=f"hb{b}")
-                nc.scalar.activation(hb[b][:].rearrange("r (u p e) -> r u p e", u=2, e=2),
-                                     banks[b][:].rearrange("r (p u e) -> r u p e", u=2, e=2), ACT.Exp)
+                for t in range(4):
+                    add_turned(tail[:, t, P * b : P * b + P], b, t, t == 3)
+                hid_t[b] = keep.tile([P, H], BF16, name=f"hid_t{b}")
+                nc.scalar.activation(hid_t[b][:].rearrange("r (c p e) -> r c p e", c=2, e=2),
+                                     banks[b][:].rearrange("r (p c e) -> r c p e", c=2, e=2), ACT.Exp)
             for i, b in enumerate(blocks):
-                for u in range(2):
-                    nc.tensor.transpose(banks[blocks[0]][:, P * (2 * i + u) : P * (2 * i + u) + P], hb[b][:].bitcast(F32)[:, P * u : P * u + P], ident[:])
+                for c in range(2):
+                    nc.tensor.transpose(banks[blocks[0]][:, P * (2 * i + c) : P * (2 * i + c) + P], hid_t[b][:].bitcast(F32)[:, P * c : P * c + P], ident[:])
 
-        def bands(q):
+        def make_bands(q):
             width = CHUNKS[q]
             bank = banks[starts[q] // P]
-            hq = keep.tile([P, 4 * width], BF16, name=f"hq{q}", align_bytes=64)
-            nc.vector.tensor_copy(hq[:].bitcast(F32).rearrange("p (b r u) -> p b r u", u=2, r=P),
-                                  bank[:, 0 : 2 * width].rearrange("p (b u r) -> p b r u", u=2, r=P))
-            hc = keep.tile([P, width], U32, name=f"hc{q}", align_bytes=64)
-            hs = keep.tile([P, width], U8, name=f"hs{q}", align_bytes=64)
-            nc.vector.quantize_mx(hc[:].bitcast(FP8X4), hs[:], hq[:])
-            nc.tensor.matmul_mx(bank[:, 0:width], w3c[:].bitcast(FP8X4), w3s[:], hc[:].bitcast(FP8X4), hs[:], start=True, stop=True)
+            hid_k = keep.tile([P, 4 * width], BF16, name=f"hid_k{q}", align_bytes=64)
+            nc.vector.tensor_copy(hid_k[:].bitcast(F32).rearrange("p (b r c) -> p b r c", c=2, r=P),
+                                  bank[:, 0 : 2 * width].rearrange("p (b c r) -> p b r c", c=2, r=P))
+            hid_codes = keep.tile([P, width], U32, name=f"hid_codes{q}", align_bytes=64)
+            hid_scales = keep.tile([P, width], U8, name=f"hid_scales{q}", align_bytes=64)
+            nc.vector.quantize_mx(hid_codes[:].bitcast(FP8X4), hid_scales[:], hid_k[:])
+            nc.tensor.matmul_mx(bank[:, 0:width], w3c[:].bitcast(FP8X4), w3s[:], hid_codes[:].bitcast(FP8X4), hid_scales[:], start=True, stop=True)
             staged = keep.tile([P, width], F32, name=f"staged{q}")
-            if q in STAGE_ON_SCALAR:
+            if q >= FIRST_CHUNK_OUT_BY_SCALAR:
                 nc.scalar.copy(staged[:], bank[:, 0:width])
             else:
                 nc.vector.tensor_copy(staged[:], bank[:, 0:width])
             nc.sync.dma_start(out[:, starts[q] : starts[q] + width], staged[:])
 
-        for t in (2, 0, 3):
-            for h in range(2):
-                s_gathers(t, h)
-        log_tables()
-        products(2)
-        l_table(0)
-        l_table(1)
-        for t in (2, 0, 3):
-            square(t)
-        for h in range(2):
-            s_gathers(1, h)
-        products(0)
-        length(2)
-        length(0)
-        products(3)
-        logs(2)
-        length(3)
-        logs(0)
-        for t, h in ((0, 0), (2, 0), (1, 0), (3, 0)):
-            l_gathers(t, h)
-            l_in(t, h)
-        logs(3)
-        products(1)
-        square(1)
-        for t, h in ((0, 1), (1, 1)):
-            l_gathers(t, h)
-            l_in(t, h)
-        length(1)
-        logs(1)
-        for t in (2, 3):
-            l_gathers(t, 1)
-            l_in(t, 1)
+        first, second, third = EARLY_PLANES
+        for t in EARLY_PLANES:
+            gather_s(t)
+        log_amp()
+        make_cross(first)
+        for pair in range(2):
+            make_logf(pair)
+        for t in EARLY_PLANES:
+            square_early(t)
+        gather_s(LAST_PLANE)
+        make_cross(second)
+        d2_early(first)
+        d2_early(second)
+        make_cross(third)
+        take_log(first)
+        d2_early(third)
+        take_log(second)
+        add_logf(second, 0, own_room(second, 0))
+        add_logf(first, 0, own_room(first, 0))
+        add_logf(LAST_PLANE, 0, halves(sq[second]))
+        add_logf(third, 0, own_room(third, 0))
+        take_log(third)
+        nc.vector.tensor_tensor(sq[LAST_PLANE][:], sa[LAST_PLANE][:], sb[LAST_PLANE][:], ALU.add)
+        make_cross(LAST_PLANE)
+        nc.scalar.activation(sq[LAST_PLANE][:], sq[LAST_PLANE][:], ACT.Square)
+        for t in range(2):
+            add_logf(t, 1, own_room(t, 1))
+        nc.vector.scalar_tensor_tensor(d2[LAST_PLANE][:], cross[LAST_PLANE], 2.0, sq[LAST_PLANE][:], ALU.mult, ALU.add)
+        take_log(LAST_PLANE)
+        add_logf(first, 1, halves(sq[LAST_PLANE]))
+        add_logf(third, 1, halves(cross[LAST_PLANE]))
+
         for step in range(len(CHUNKS) + 2):
             if step < len(CHUNKS):
-                root_term(step)
+                make_tail(step)
             if 1 <= step <= len(CHUNKS):
-                hidden(step - 1)
+                make_hidden(step - 1)
             if step >= 2:
-                bands(step - 2)
+                make_bands(step - 2)

import math
from contextlib import ExitStack

import concourse.mybir as mybir
from concourse.masks import make_identity

F32 = mybir.dt.float32
BF16 = mybir.dt.bfloat16
I32 = mybir.dt.int32
U32 = mybir.dt.uint32
U16 = mybir.dt.uint16
U8 = mybir.dt.uint8
FP8X4 = mybir.dt.float8_e4m3fn_x4
ACT = mybir.ActivationFunctionType
ALU = mybir.AluOpType

P = 128
K, T, S, N, H, U = 512, 1024, 512, 128, 512, 1024
FLOPS = 2 * (2 * K * H * S + H * N * U)
HALF = U // 2
W_COLS = 256
TINY = 2.0 ** -60
EARLY_PLANES = (2, 0, 3)
LAST_PLANE = 1
CHUNKS = (128, 256, 256, 256, 128)
FIRST_CHUNK_OUT_BY_SCALAR = 2


def tile_picked_ysgprd_int_p_kernel(tc, x_words, x_scales, w1, w2, cos, unit, w3, offs, la, lb, out):
    nc = tc.nc
    with ExitStack() as ctx:
        keep = ctx.enter_context(tc.tile_pool(name="keep", bufs=1))
        psum = ctx.enter_context(tc.psum_pool(name="psum", bufs=1))
        banks = [psum.tile([P, HALF], F32, name=f"bank{b}") for b in range(8)]

        offs_t = keep.tile([P, S // 16], U16, name="offs_t")
        la_t = keep.tile([P, U // 16], U16, name="la_t")
        lb_t = keep.tile([P, U // 16], U16, name="lb_t")
        xw = keep.tile([P, T], I32, name="xw")
        xs = keep.tile([P, T], U8, name="xs")
        nc.sync.dma_start(offs_t[:], offs)
        for q in range(4):
            rows = x_scales[0, 4 * q : 4 * q + 4, :].bitcast(I32).unsqueeze(0).to_broadcast([8, 4, T // 4])
            (nc.sync if q < 2 else nc.scalar).dma_start(xs[32 * q : 32 * q + 32, :].bitcast(I32), rows)
        nc.sync.dma_start(xw[:], x_words[0].rearrange("p n t -> p (n t)").bitcast(I32))
        raws = []
        for wi, w in enumerate((w1, w2)):
            for side in range(2):
                raw = keep.tile([P, 4, W_COLS], F32, name=f"raw{wi}{side}")
                nc.sync.dma_start(raw[:], w.rearrange("(p j) c -> p j c", j=4)[:, :, W_COLS * side : W_COLS * side + W_COLS])
                raws.append(raw)
        nc.sync.dma_start(la_t[:], la)
        nc.sync.dma_start(lb_t[:], lb)
        unit_t = keep.tile([P, 4], F32, name="unit_t")
        unit_k = keep.tile([P, 4], F32, name="unit_k")
        w3raw = keep.tile([P, 4, N], F32, name="w3raw")
        nc.sync.dma_start(unit_k[:], unit.rearrange("(p j) o -> p (j o)", j=4))
        with nc.allow_non_contiguous_dma(reason="one value a partition and plane"):
            nc.sync.dma_start(unit_t[:], unit.rearrange("(t p) o -> p (t o)", p=P))
        nc.sync.dma_start(w3raw[:], w3.rearrange("(p j) n -> p j n", j=4))
        cos_t = {}
        for t in EARLY_PLANES + (LAST_PLANE,):
            cos_t[t] = keep.tile([P, U], F32, name=f"cos{t}")
            nc.sync.dma_start(cos_t[t][:], cos[P * t : P * t + P, :])
        ident = keep.tile([P, P], F32, name="ident")
        make_identity(nc, ident[:])

        xg = keep.tile([P, S], U32, name="xg", align_bytes=64)
        xsg = keep.tile([P, S], U8, name="xsg", align_bytes=64)
        nc.vector.tensor_copy(xsg[:], xs[:].indirect(offs_t[:]))
        nc.vector.tensor_copy(xg[:], xw[:].bitcast(U32).indirect(offs_t[:]))

        s_tab = [keep.tile([P, 3 * S], F32, name="s_tab0"), keep.tile([P, 3 * S], F32, name="s_tab1")]
        logf_tab = [keep.tile([P, 3 * S], F32, name="logf_tab0"), keep.tile([P, 3 * S], F32, name="logf_tab1")]
        work = [keep.tile([P, 2 * S], F32, name="work0"), keep.tile([P, 2 * S], F32, name="work1")]
        exp_ya = [tab[:, 2 * S : 3 * S] for tab in s_tab + logf_tab]

        def work_plane(t):
            return work[t % 2][:, S * (t // 2) : S * (t // 2) + S]

        for ci, raw in enumerate(raws):
            wi, side = divmod(ci, 2)
            grouped = keep.tile([P, W_COLS, 4], BF16, name=f"grouped{ci}", align_bytes=64)
            nc.vector.tensor_copy(grouped[:].rearrange("p (c i) j -> p c j i", i=4), raw[:].rearrange("p j (c i) -> p c j i", i=4))
            codes = keep.tile([P, W_COLS], U32, name=f"codes{ci}", align_bytes=64)
            scales = keep.tile([P, W_COLS], U8, name=f"scales{ci}", align_bytes=64)
            nc.vector.quantize_mx(codes[:].bitcast(FP8X4), scales[:], grouped[:].rearrange("p c j -> p (c j)"))
            for i in range(2):
                t = 2 * side + i
                y = banks[4 * wi + t]
                nc.tensor.matmul_mx(y[:], codes[:, P * i : P * i + P].bitcast(FP8X4), scales[:, P * i : P * i + P],
                                    xg[:].bitcast(FP8X4), xsg[:], start=True, stop=True)
                nc.scalar.activation(exp_ya[t] if wi == 0 else work_plane(t), y[:], ACT.Exp)

        sgn = keep.tile([P, 4], F32, name="sgn")
        nc.vector.tensor_scalar(sgn[:], unit_k[:], 0.0, 2.0, ALU.is_ge, ALU.mult)
        nc.vector.tensor_scalar(sgn[:], sgn[:], -1.0, None, ALU.add)
        root = keep.tile([P, 4], F32, name="root")
        one_half = keep.tile([P, 4], F32, name="one_half")
        nc.gpsimd.memset(one_half[:], 0.5)
        nc.vector.scalar_tensor_tensor(unit_t[:], unit_t[:], -1.0, unit_t[:], ALU.mult, ALU.max)
        nc.gpsimd.tensor_tensor(root[:], unit_t[:], one_half[:], ALU.pow)
        w3g = keep.tile([P, N, 4], BF16, name="w3g", align_bytes=64)
        nc.vector.tensor_tensor(w3g[:], w3raw[:].rearrange("p j n -> p n j"), sgn[:].unsqueeze(1).to_broadcast([P, N, 4]), ALU.mult)
        w3c = keep.tile([P, N], U32, name="w3c", align_bytes=64)
        w3s = keep.tile([P, N], U8, name="w3s", align_bytes=64)
        nc.vector.quantize_mx(w3c[:].bitcast(FP8X4), w3s[:], w3g[:].rearrange("p n j -> p (n j)"))

        for pair in range(2):
            nc.scalar.activation(s_tab[pair][:, 0 : 2 * S], work[pair][:], ACT.Ln, bias=math.exp(0.4), scale=math.exp(0.4))

        sa = {t: keep.tile([P, U], F32, name=f"sa{t}") for t in range(4)}
        sb = {t: keep.tile([P, U], F32, name=f"sb{t}") for t in range(4)}
        tail = keep.tile([P, 4, U], F32, name="tail")
        cross = {t: keep.tile([P, U], F32, name="cross_last")[:] if t == LAST_PLANE else tail[:, t, :] for t in range(4)}
        sq = {t: keep.tile([P, U], F32, name=f"sq{t}") for t in range(4)}
        d2 = {t: keep.tile([P, U], F32, name=f"d2{t}") for t in range(4)}
        log_d2 = keep.tile([P, 4, U], F32, name="log_d2")

        def half_cols(h):
            return slice(HALF * h, HALF * h + HALF)

        def gather(dst, tabs, t, lst, h, on_scalar):
            window = tabs[t][:] if t < 2 else tabs[t - 2][:, S : 3 * S]
            picked = window.indirect(lst[:, 32 * h : 32 * h + 32])
            if on_scalar:
                nc.scalar.activation(dst, picked, ACT.Copy)
            else:
                nc.vector.tensor_copy(dst, picked)

        def gather_s(t):
            for h in range(2):
                gather(sa[t][:, half_cols(h)], s_tab, t, la_t, h, t < 2)
                gather(sb[t][:, half_cols(h)], s_tab, t, lb_t, h, t < 2)

        def log_amp():
            for t in range(4):
                nc.scalar.activation(work_plane(t), exp_ya[t], ACT.Ln, bias=1.0)
            for t in (0, 2, 1, 3):
                nc.scalar.activation(work_plane(t), work_plane(t), ACT.Ln, bias=TINY, scale=root[:, t : t + 1])

        def make_logf(pair):
            nc.vector.scalar_tensor_tensor(logf_tab[pair][:, 0 : 2 * S], s_tab[pair][:, 0 : 2 * S], -0.7, work[pair][:], ALU.mult, ALU.add)

        def make_cross(t):
            nc.vector.tensor_tensor(cross[t], sa[t][:], sb[t][:], ALU.mult)
            nc.vector.scalar_tensor_tensor(cross[t], cos_t[t][:], -1.0, cross[t], ALU.add, ALU.mult)

        def sum_bank(t, h):
            return banks[2 * EARLY_PLANES.index(t) + h]

        def square_early(t):
            for h in range(2):
                bank = sum_bank(t, h)
                for b in range(4):
                    block = slice(HALF * h + P * b, HALF * h + P * b + P)
                    nc.tensor.matmul(bank[:, P * b : P * b + P], sa[t][:, block], ident[:], start=True, stop=False, is_transpose=True)
                    nc.tensor.matmul(bank[:, P * b : P * b + P], sb[t][:, block], ident[:], start=False, stop=True, is_transpose=True)
                nc.scalar.activation(sq[t][:, half_cols(h)], bank[:], ACT.Square)
                for b in range(4):
                    nc.tensor.transpose(bank[:, P * b : P * b + P], sq[t][:, HALF * h + P * b : HALF * h + P * b + P], ident[:])

        def d2_early(t):
            for h in range(2):
                nc.vector.scalar_tensor_tensor(d2[t][:, half_cols(h)], cross[t][:, half_cols(h)], 2.0, sum_bank(t, h)[:], ALU.mult, ALU.add)

        def take_log(t):
            nc.scalar.activation(log_d2[:, t, :], d2[t][:], ACT.Ln, bias=0.1)

        opened = set()

        def add_turned(term, b, t, last):
            nc.tensor.matmul(banks[b][:, P * t : P * t + P], term, ident[:], start=b not in opened, stop=last, is_transpose=True)
            opened.add(b)

        def add_logf(t, h, room):
            gather(room[0], logf_tab, t, la_t, h, t < 2)
            gather(room[1], logf_tab, t, lb_t, h, t < 2 and (t, h) != (LAST_PLANE, 1))
            for b in range(4):
                for term in room:
                    add_turned(term[:, P * b : P * b + P], 4 * h + b, t, False)

        def own_room(t, h):
            return sa[t][:, half_cols(h)], sb[t][:, half_cols(h)]

        def halves(region):
            return region[:, half_cols(0)], region[:, half_cols(1)]

        starts = [sum(CHUNKS[:q]) for q in range(len(CHUNKS))]

        def make_tail(q):
            cols = slice(starts[q], starts[q] + CHUNKS[q])
            nc.scalar.activation(tail[:, :, cols], log_d2[:, :, cols], ACT.Exp, bias=math.log(0.7), scale=0.5)
            nc.vector.scalar_tensor_tensor(tail[:, :, cols], log_d2[:, :, cols], -0.5, tail[:, :, cols], ALU.mult, ALU.add)

        def make_hidden(q):
            blocks = range(starts[q] // P, (starts[q] + CHUNKS[q]) // P)
            hid_t = {}
            for b in blocks:
                for t in range(4):
                    add_turned(tail[:, t, P * b : P * b + P], b, t, t == 3)
                hid_t[b] = keep.tile([P, H], BF16, name=f"hid_t{b}")
                nc.scalar.activation(hid_t[b][:].rearrange("r (c p e) -> r c p e", c=2, e=2),
                                     banks[b][:].rearrange("r (p c e) -> r c p e", c=2, e=2), ACT.Exp)
            for i, b in enumerate(blocks):
                for c in range(2):
                    nc.tensor.transpose(banks[blocks[0]][:, P * (2 * i + c) : P * (2 * i + c) + P], hid_t[b][:].bitcast(F32)[:, P * c : P * c + P], ident[:])

        def make_bands(q):
            width = CHUNKS[q]
            bank = banks[starts[q] // P]
            hid_k = keep.tile([P, 4 * width], BF16, name=f"hid_k{q}", align_bytes=64)
            nc.vector.tensor_copy(hid_k[:].bitcast(F32).rearrange("p (b r c) -> p b r c", c=2, r=P),
                                  bank[:, 0 : 2 * width].rearrange("p (b c r) -> p b r c", c=2, r=P))
            hid_codes = keep.tile([P, width], U32, name=f"hid_codes{q}", align_bytes=64)
            hid_scales = keep.tile([P, width], U8, name=f"hid_scales{q}", align_bytes=64)
            nc.vector.quantize_mx(hid_codes[:].bitcast(FP8X4), hid_scales[:], hid_k[:])
            nc.tensor.matmul_mx(bank[:, 0:width], w3c[:].bitcast(FP8X4), w3s[:], hid_codes[:].bitcast(FP8X4), hid_scales[:], start=True, stop=True)
            staged = keep.tile([P, width], F32, name=f"staged{q}")
            if q >= FIRST_CHUNK_OUT_BY_SCALAR:
                nc.scalar.copy(staged[:], bank[:, 0:width])
            else:
                nc.vector.tensor_copy(staged[:], bank[:, 0:width])
            nc.sync.dma_start(out[:, starts[q] : starts[q] + width], staged[:])

        first, second, third = EARLY_PLANES
        for t in EARLY_PLANES:
            gather_s(t)
        log_amp()
        make_cross(first)
        for pair in range(2):
            make_logf(pair)
        for t in EARLY_PLANES:
            square_early(t)
        gather_s(LAST_PLANE)
        make_cross(second)
        d2_early(first)
        d2_early(second)
        make_cross(third)
        take_log(first)
        d2_early(third)
        take_log(second)
        add_logf(second, 0, own_room(second, 0))
        add_logf(first, 0, own_room(first, 0))
        add_logf(LAST_PLANE, 0, halves(sq[second]))
        add_logf(third, 0, own_room(third, 0))
        take_log(third)
        nc.vector.tensor_tensor(sq[LAST_PLANE][:], sa[LAST_PLANE][:], sb[LAST_PLANE][:], ALU.add)
        make_cross(LAST_PLANE)
        nc.scalar.activation(sq[LAST_PLANE][:], sq[LAST_PLANE][:], ACT.Square)
        for t in range(2):
            add_logf(t, 1, own_room(t, 1))
        nc.vector.scalar_tensor_tensor(d2[LAST_PLANE][:], cross[LAST_PLANE], 2.0, sq[LAST_PLANE][:], ALU.mult, ALU.add)
        take_log(LAST_PLANE)
        add_logf(first, 1, halves(sq[LAST_PLANE]))
        add_logf(third, 1, halves(cross[LAST_PLANE]))

        for step in range(len(CHUNKS) + 2):
            if step < len(CHUNKS):
                make_tail(step)
            if 1 <= step <= len(CHUNKS):
                make_hidden(step - 1)
            if step >= 2:
                make_bands(step - 2)
